import numpy as np
import ml_dtypes


def mxq(x, axis, fmt="e4m3"):
    dtype, down = {"e4m3": (ml_dtypes.float8_e4m3fn, 7), "e5m2": (ml_dtypes.float8_e5m2, 14)}[fmt]
    v = np.moveaxis(np.asarray(x, np.float32).astype(ml_dtypes.bfloat16).astype(np.float64), axis, -1)
    blocks = v.reshape(v.shape[:-1] + (-1, 32))
    amax = np.abs(blocks).max(-1, keepdims=True)
    byte = np.maximum(np.where(amax > 0, np.frexp(amax)[1] - 1 + 127, 0) - down, 1)
    scale = np.exp2(byte - 127.0)
    codes = (blocks / scale).astype(np.float32).astype(dtype).astype(np.float64)
    return np.moveaxis((codes * scale).reshape(v.shape), -1, axis)


WIDE = False


def mx_kscale(k):
    if not WIDE:
        return np.ones(k)
    levels = np.array([10, -10, 5, -5, 0])
    if k % 512:
        return np.exp2(np.random.permutation(np.resize(levels, k // 32))).repeat(32)
    a = np.empty((k // 512, 16))
    for p in range(k // 512):
        a[p, :8] = np.random.permutation(np.resize(levels, 8))
        for g in range(8):
            far = levels[np.abs(levels - a[p, g]) >= 10]
            a[p, g + 8] = far[np.random.randint(len(far))]
    return np.exp2(a.ravel()).repeat(32)


def f64(x):
    return np.asarray(x).astype(np.float64)


def striped(idx):
    return np.tile(np.asarray(idx).reshape(-1, 16).T, (8, 1)).astype(np.uint16)


def unstriped(offs):
    return offs[:16].T.reshape(-1).astype(np.int64)


E2M1 = np.array([0.0, 0.5, 1.0, 1.5, 2.0, 3.0, 4.0, 6.0, -0.0, -0.5, -1.0, -1.5, -2.0, -3.0, -4.0, -6.0])


def pack_weight(w, fmt):
    k, n = w.shape
    w = f64(np.asarray(w, np.float32).astype(ml_dtypes.bfloat16)).reshape(k // 32, 32, n)
    amax = np.abs(w).max(1)
    if fmt == "e4m3":
        byte = np.frexp(amax)[1] - 1 + 127 - 7
    else:
        mant, ex = np.frexp(amax / 6.0)
        byte = np.where(mant > 0.5, ex, ex - 1) + 127
    byte = np.clip(np.where(amax > 0, byte, 1), 1, 254)
    scaled = (w * np.exp2(127.0 - byte)[:, None, :]).reshape(k, n).astype(np.float32)
    by_word = np.ascontiguousarray(scaled.reshape(k // 512, 128, 4, n).transpose(0, 1, 3, 2))
    if fmt == "e4m3":
        words = by_word.astype(ml_dtypes.float8_e4m3fn).view(np.uint8)
    else:
        c = by_word.astype(ml_dtypes.float4_e2m1fn).view(np.uint8) & 0xF
        words = (c[..., 0::2] | (c[..., 1::2] << 4)).reshape(k // 512, 128, 2 * n)
    return np.ascontiguousarray(words), np.ascontiguousarray(byte.astype(np.uint8).reshape(k // 512, 16, n))


def unpack_weight(words, scales, fmt):
    g, _, n = scales.shape
    words = np.ascontiguousarray(words).reshape(g, 128, n, -1)
    if fmt == "e4m3":
        vals = words.view(ml_dtypes.float8_e4m3fn).astype(np.float64)
    else:
        nib = np.empty((g, 128, n, 4), np.uint8)
        nib[..., 0::2] = words & 0xF
        nib[..., 1::2] = words >> 4
        vals = E2M1[nib]
    vals = vals * np.repeat(np.exp2(scales.astype(np.float64) - 127.0), 8, axis=1)[..., None]
    return vals.transpose(0, 1, 3, 2).reshape(g * 512, n)


D, T, I, Q, E, M = 512, 1024, 512, 512, 512, 1024


def setup_inputs():
    n = np.random.standard_normal
    idx = np.random.permutation(T)[:I]
    idx2 = np.random.permutation(T)[:I]
    idx3 = np.random.permutation(T)[:I]
    idx4 = np.random.permutation(M)[:I]
    fd = mx_kscale(D)
    fq = mx_kscale(Q)
    keysp = pack_weight(n((D, T)) / fd[:, None], "e4m3")
    return {
        "query": (n((D, Q)) * 0.9 / np.sqrt(D) * fd[:, None]).astype(np.float32),
        "keys_words": keysp[0],
        "keys_scales": keysp[1],
        "lam": (np.random.uniform(0.3, 0.9, (Q, 1))).astype(np.float32),
        "qs": (np.random.uniform(0.5, 2.0, (Q, 1)) * fq[:, None]).astype(np.float32),
        "msgs": (n((Q, E)) * 1 / np.sqrt(Q) / fq[:, None]).astype(np.float32),
        "old": (n((E, M)) * 1.0).astype(np.float32),
        "fade": (np.random.uniform(0.3, 0.9, (1, M))).astype(np.float32),
        "offs": striped(idx),
        "offs2": striped(idx2),
        "offs3": striped(idx3),
        "offs4": striped(idx4),
    }


def reference(query, keys_words, keys_scales, lam, qs, msgs, old, fade, offs, offs2, offs3, offs4):
    idx = unstriped(offs)
    idx2 = unstriped(offs2)
    idx3 = unstriped(offs3)
    idx4 = unstriped(offs4)
    keysu = unpack_weight(keys_words, keys_scales, "e4m3")
    queryq = mxq(f64(query), 0, "e4m3")
    a = queryq.T @ keysu
    w = a[:, idx] + np.maximum(a[:, idx2], a[:, idx3]) * f64(lam)
    wq = w * f64(qs)
    msgsq = mxq(f64(msgs), 0, "e4m3")
    wqq = mxq(wq, 0, "e4m3")
    dl = msgsq.T @ wqq
    df = np.zeros((E, M))
    df[:, idx4] = dl
    y = f64(old) * f64(fade) + df
    return y

@@ -1,0 +1,198 @@
+from contextlib import ExitStack
+
+import concourse.mybir as mybir
+
+D, T, I, Q, E, M = 512, 1024, 512, 512, 512, 1024
+FLOPS = 2 * D * Q * T + 2 * Q * E * I
+
+F32 = mybir.dt.float32
+BF16 = mybir.dt.bfloat16
+I32 = mybir.dt.int32
+U32 = mybir.dt.uint32
+U16 = mybir.dt.uint16
+U8 = mybir.dt.uint8
+FP8X4 = mybir.dt.float8_e4m3fn_x4
+ALU = mybir.AluOpType
+COPY = mybir.ActivationFunctionType.Copy
+
+P = 128
+PACK = 4
+BANK = 512
+HALF = I // 2
+LIST_COLS = HALF // 16
+
+
+def tile_attend_lookahead_delivered_lean_kernel(tc, query, keys_words, keys_scales, lam, qs, msgs, old, fade, offs, offs2, offs3, offs4, out):
+    nc = tc.nc
+    with ExitStack() as ctx:
+        sb = ctx.enter_context(tc.tile_pool(name="sb", bufs=1))
+        ps = ctx.enter_context(tc.psum_pool(name="ps", bufs=1))
+
+        def tile(shape, dtype, name):
+            return sb.tile(shape, dtype, name=name, align_bytes=64)
+
+        def move(engine, dst, src):
+            if engine == "S":
+                nc.scalar.activation(dst, src, COPY)
+            else:
+                nc.vector.tensor_copy(dst, src)
+
+        key_plane = tile([P, T], U8, "key_plane")
+        nc.vector.memset(key_plane[:].bitcast(I32), 0)
+        q_raw = [tile([P, PACK, Q // 2], F32, f"q_raw{u}") for u in range(2)]
+        for u in range(2):
+            nc.sync.dma_start(q_raw[u][:], query.rearrange("(p j) c -> p j c", j=PACK)[:, :, u * (Q // 2) : (u + 1) * (Q // 2)])
+        for g in range(4):
+            nc.scalar.dma_start(key_plane[32 * g : 32 * g + 4, :].bitcast(I32), keys_scales[0, 4 * g : 4 * g + 4, :].bitcast(I32))
+        key_words = tile([P, T], U32, "key_words")
+        nc.sync.dma_start(key_words[:].bitcast(I32), keys_words[0].rearrange("p n t -> p (n t)").bitcast(I32))
+        lists = [tile([P, I // 16], U16, f"list{k}") for k in range(4)]
+        for k, src in ((1, offs2), (2, offs3), (0, offs)):
+            nc.sync.dma_start(lists[k][:], src)
+        lam4 = tile([P, PACK], F32, "lam4")
+        qs4 = tile([P, PACK], F32, "qs4")
+        nc.sync.dma_start(lam4[:], lam.rearrange("(p j) o -> p (j o)", j=PACK))
+        nc.sync.dma_start(qs4[:], qs.rearrange("(p j) o -> p (j o)", j=PACK))
+        m_raw = tile([P, PACK, E], F32, "m_raw")
+        nc.sync.dma_start(m_raw[:], msgs.rearrange("(p j) c -> p j c", j=PACK))
+        nc.sync.dma_start(lists[3][:], offs4)
+        fade_all = tile([P, M], F32, "fade_all")
+        nc.sync.dma_start(fade_all[:], fade.rearrange("o m -> (o m)").partition_broadcast(P))
+        old_sb = [tile([P, M], F32, f"old{e}") for e in range(4)]
+        for e in range(4):
+            nc.sync.dma_start(old_sb[e][:], old[e * P : (e + 1) * P, :])
+
+        df = [tile([P, M], F32, f"df{e}") for e in range(4)]
+        for e in range(4):
+            nc.vector.memset(df[e][:], 0.0)
+
+        q_bf = tile([P, Q * PACK], BF16, "q_bf")
+        q_view = q_bf[:].rearrange("p (r m j) -> p m j r", r=PACK, j=PACK)
+        for u in range(2):
+            nc.vector.tensor_copy(q_view[:, u * 64 : (u + 1) * 64], q_raw[u][:].rearrange("p j (m r) -> p m j r", r=PACK))
+        q_codes = [tile([P, P], U32, f"q_codes{r}") for r in range(PACK)]
+        q_plane = [tile([P, P], U8, f"q_plane{r}") for r in range(PACK)]
+        for r in range(PACK):
+            nc.vector.quantize_mx(q_codes[r][:].bitcast(FP8X4), q_plane[r][:], q_bf[:, r * 512 : (r + 1) * 512])
+
+        a = [tile([P, T], F32, f"a{r}") for r in range(PACK)]
+        banks = [ps.tile([P, BANK], F32, name=f"bank{b}") for b in range(8)]
+
+        def score(r, b, engine):
+            bank = banks[2 * r + b]
+            cols = slice(b * BANK, (b + 1) * BANK)
+            nc.tensor.matmul_mx(bank[:], lhsT=q_codes[r][:].bitcast(FP8X4), lhsT_scale=q_plane[r][:],
+                                rhs=key_words[:, cols].bitcast(FP8X4), rhs_scale=key_plane[:, cols], start=True, stop=True)
+            move(engine, a[r][:, cols], bank[:])
+
+        got = {(h, r, k): tile([P, HALF], F32, f"got{h}{r}{k}") for h in range(2) for r in range(PACK) for k in range(3)}
+        wq_rows = [tile([P, PACK * HALF], BF16, f"wq_rows{h}") for h in range(2)]
+        wq_bf = [tile([P, PACK * HALF], BF16, f"wq_bf{h}") for h in range(2)]
+        wq_codes = [tile([P, HALF], U32, f"wq_codes{h}") for h in range(2)]
+        wq_plane = [tile([P, HALF], U8, f"wq_plane{h}") for h in range(2)]
+        best = {(h, r): tile([P, HALF], F32, f"best{h}{r}") for h in range(2) for r in range(PACK)}
+        w = {(h, r): tile([P, HALF], F32, f"w{h}{r}") for h in range(2) for r in range(PACK)}
+
+        def gather(h, r, k, engine):
+            move(engine, got[h, r, k][:], a[r][:].indirect(lists[k][:, h * LIST_COLS : (h + 1) * LIST_COLS]))
+
+        def gathers(h, r, engine):
+            for k in (1, 2, 0):
+                gather(h, r, k, engine)
+
+        def weigh_max(h, r):
+            nc.vector.tensor_tensor(best[h, r][:], got[h, r, 1][:], got[h, r, 2][:], ALU.max)
+
+        def weigh_sum(h, r):
+            nc.vector.scalar_tensor_tensor(w[h, r][:], best[h, r][:], lam4[:, r : r + 1], got[h, r, 0][:], ALU.mult, ALU.add)
+
+        def weigh_scale(h, r):
+            nc.vector.tensor_scalar(wq_rows[h][:, r * HALF : (r + 1) * HALF], w[h, r][:], qs4[:, r : r + 1], None, ALU.mult)
+
+        def weigh(h, r):
+            weigh_max(h, r)
+            weigh_sum(h, r)
+            weigh_scale(h, r)
+
+        def interleave(dst, src, width):
+            nc.vector.tensor_copy(dst.rearrange("p (c i j) -> p c j i", i=4, j=PACK), src.rearrange("p (j c i) -> p c j i", i=4, j=PACK))
+
+        m_bf = tile([P, E * PACK], BF16, "m_bf")
+        m_codes = tile([P, E], U32, "m_codes")
+        m_plane = tile([P, E], U8, "m_plane")
+        dl = {(h, e): tile([P, 2 * HALF], F32, f"dl{h}{e}") for h in range(2) for e in range(2)}
+
+        def deliver(h):
+            interleave(wq_bf[h][:], wq_rows[h][:], HALF)
+            nc.vector.quantize_mx(wq_codes[h][:].bitcast(FP8X4), wq_plane[h][:], wq_bf[h][:])
+            for e in range(4):
+                bank = banks[2 * h + e // 2]
+                cols = slice(e * P, (e + 1) * P)
+                nc.tensor.matmul_mx(bank[:, (e % 2) * HALF : (e % 2 + 1) * HALF], lhsT=m_codes[:, cols].bitcast(FP8X4), lhsT_scale=m_plane[:, cols],
+                                    rhs=wq_codes[h][:].bitcast(FP8X4), rhs_scale=wq_plane[h][:], start=True, stop=True)
+
+        def evacuate(h, pair, engine):
+            move(engine, dl[h, pair][:], banks[2 * h + pair][:])
+
+        def scatter(h, e, engine):
+            move(engine, df[e][:].indirect(lists[3][:, h * LIST_COLS : (h + 1) * LIST_COLS]), dl[h, e // 2][:, (e % 2) * HALF : (e % 2 + 1) * HALF])
+
+        faded = [tile([P, M], F32, f"faded{e}") for e in range(4)]
+        res = [tile([P, M], F32, f"res{e}") for e in range(4)]
+
+        def fade_old(e):
+            nc.vector.tensor_tensor(faded[e][:], old_sb[e][:], fade_all[:], ALU.mult)
+
+        def finish(e, pieces):
+            width = M // pieces
+            for c in range(pieces):
+                cols = slice(c * width, (c + 1) * width)
+                nc.vector.tensor_tensor(res[e][:, cols], faded[e][:, cols], df[e][:, cols], ALU.add)
+                nc.sync.dma_start(out[e * P : (e + 1) * P, cols], res[e][:, cols])
+
+        def unit(h, r):
+            gather(h, r, 1, "S")
+            gather(h, r, 2, "S")
+            gather(h, r, 0, "V")
+        for r in range(PACK):
+            score(r, 0, "S")
+            score(r, 1, "V")
+            if r >= 1:
+                unit(0, r - 1)
+            if r >= 2:
+                weigh(0, r - 2)
+        unit(0, 3)
+        interleave(m_bf[:], m_raw[:].rearrange("p j c -> p (j c)"), E)
+        weigh(0, 2)
+        nc.vector.quantize_mx(m_codes[:].bitcast(FP8X4), m_plane[:], m_bf[:])
+        unit(1, 0)
+        weigh(0, 3)
+        unit(1, 1)
+        deliver(0)
+        weigh(1, 0)
+        unit(1, 2)
+        weigh(1, 1)
+        unit(1, 3)
+        weigh(1, 2)
+        evacuate(0, 0, "S")
+        scatter(0, 0, "S")
+        weigh(1, 3)
+        deliver(1)
+        fade_old(0)
+        scatter(0, 1, "S")
+        evacuate(1, 0, "V")
+        scatter(1, 0, "V")
+        evacuate(0, 1, "S")
+        scatter(1, 1, "S")
+        finish(0, 1)
+        fade_old(1)
+        scatter(0, 2, "S")
+        evacuate(1, 1, "V")
+        finish(1, 1)
+        scatter(1, 2, "S")
+        fade_old(2)
+        fade_old(3)
+        scatter(0, 3, "S")
+        finish(2, 1)
+        scatter(1, 3, "S")
+        finish(3, 2)

@@ -47,20 +47,21 @@ def tile_attend_lookahead_delivered_lean_kernel(tc, query, keys_words, keys_scal
         key_words = tile([P, T], U32, "key_words")
         nc.sync.dma_start(key_words[:].bitcast(I32), keys_words[0].rearrange("p n t -> p (n t)").bitcast(I32))
         lists = [tile([P, I // 16], U16, f"list{k}") for k in range(4)]
-        for k, src in ((1, offs2), (2, offs3), (0, offs)):
+        for k, src in ((1, offs2), (0, offs), (2, offs3)):
             nc.sync.dma_start(lists[k][:], src)
         lam4 = tile([P, PACK], F32, "lam4")
         qs4 = tile([P, PACK], F32, "qs4")
-        nc.sync.dma_start(lam4[:], lam.rearrange("(p j) o -> p (j o)", j=PACK))
-        nc.sync.dma_start(qs4[:], qs.rearrange("(p j) o -> p (j o)", j=PACK))
         m_raw = tile([P, PACK, E], F32, "m_raw")
         nc.sync.dma_start(m_raw[:], msgs.rearrange("(p j) c -> p j c", j=PACK))
-        nc.sync.dma_start(lists[3][:], offs4)
         fade_all = tile([P, M], F32, "fade_all")
         nc.sync.dma_start(fade_all[:], fade.rearrange("o m -> (o m)").partition_broadcast(P))
         old_sb = [tile([P, M], F32, f"old{e}") for e in range(4)]
         for e in range(4):
             nc.sync.dma_start(old_sb[e][:], old[e * P : (e + 1) * P, :])
+            if e == 1:
+                nc.sync.dma_start(lam4[:], lam.rearrange("(p j) o -> p (j o)", j=PACK))
+                nc.sync.dma_start(qs4[:], qs.rearrange("(p j) o -> p (j o)", j=PACK))
+                nc.sync.dma_start(lists[3][:], offs4)
 
         df = [tile([P, M], F32, f"df{e}") for e in range(4)]
         for e in range(4):
@@ -85,34 +86,34 @@ def tile_attend_lookahead_delivered_lean_kernel(tc, query, keys_words, keys_scal
                                 rhs=key_words[:, cols].bitcast(FP8X4), rhs_scale=key_plane[:, cols], start=True, stop=True)
             move(engine, a[r][:, cols], bank[:])
 
-        got = {(h, r, k): tile([P, HALF], F32, f"got{h}{r}{k}") for h in range(2) for r in range(PACK) for k in range(3)}
+        own = [tile([P, I], F32, f"own{r}") for r in range(PACK)]
+        got = {}
         wq_rows = [tile([P, PACK * HALF], BF16, f"wq_rows{h}") for h in range(2)]
-        wq_bf = [tile([P, PACK * HALF], BF16, f"wq_bf{h}") for h in range(2)]
+        wq_bf = [tile([P, PACK * HALF], BF16, ("wq_bf0", "late")[h]) for h in range(2)]
         wq_codes = [tile([P, HALF], U32, f"wq_codes{h}") for h in range(2)]
         wq_plane = [tile([P, HALF], U8, f"wq_plane{h}") for h in range(2)]
-        best = {(h, r): tile([P, HALF], F32, f"best{h}{r}") for h in range(2) for r in range(PACK)}
+        best = {}
         w = {(h, r): tile([P, HALF], F32, f"w{h}{r}") for h in range(2) for r in range(PACK)}
 
         def gather(h, r, k, engine):
-            move(engine, got[h, r, k][:], a[r][:].indirect(lists[k][:, h * LIST_COLS : (h + 1) * LIST_COLS]))
+            if r == 0:
+                got.setdefault((h, k), tile([P, PACK * HALF], F32, (f"got{k}", ("key_words", "key_plane")[k - 1])[h]))
+            move(engine, got[h, k][:, r * HALF : (r + 1) * HALF], a[r][:].indirect(lists[k][:, h * LIST_COLS : (h + 1) * LIST_COLS]))
 
-        def gathers(h, r, engine):
-            for k in (1, 2, 0):
-                gather(h, r, k, engine)
+        def gather_own(r):
+            nc.vector.tensor_copy(own[r][:], a[r][:].indirect(lists[0][:]))
 
-        def weigh_max(h, r):
-            nc.vector.tensor_tensor(best[h, r][:], got[h, r, 1][:], got[h, r, 2][:], ALU.max)
+        def weigh_max(h, pair):
+            if pair == 0:
+                best.setdefault(h, tile([P, PACK * HALF], F32, ("m_bf", "wq_bf0")[h]))
+            cols = slice(2 * pair * HALF, 2 * (pair + 1) * HALF)
+            nc.vector.tensor_tensor(best[h][:, cols], got[h, 1][:, cols], got[h, 2][:, cols], ALU.max)
 
         def weigh_sum(h, r):
-            nc.vector.scalar_tensor_tensor(w[h, r][:], best[h, r][:], lam4[:, r : r + 1], got[h, r, 0][:], ALU.mult, ALU.add)
+            nc.vector.scalar_tensor_tensor(w[h, r][:], best[h][:, r * HALF : (r + 1) * HALF], lam4[:, r : r + 1], own[r][:, h * HALF : (h + 1) * HALF], ALU.mult, ALU.add)
 
         def weigh_scale(h, r):
             nc.vector.tensor_scalar(wq_rows[h][:, r * HALF : (r + 1) * HALF], w[h, r][:], qs4[:, r : r + 1], None, ALU.mult)
-
-        def weigh(h, r):
-            weigh_max(h, r)
-            weigh_sum(h, r)
-            weigh_scale(h, r)
 
         def interleave(dst, src, width):
             nc.vector.tensor_copy(dst.rearrange("p (c i j) -> p c j i", i=4, j=PACK), src.rearrange("p (j c i) -> p c j i", i=4, j=PACK))
@@ -123,7 +124,6 @@ def tile_attend_lookahead_delivered_lean_kernel(tc, query, keys_words, keys_scal
         dl = {(h, e): tile([P, 2 * HALF], F32, f"dl{h}{e}") for h in range(2) for e in range(2)}
 
         def deliver(h):
-            interleave(wq_bf[h][:], wq_rows[h][:], HALF)
             nc.vector.quantize_mx(wq_codes[h][:].bitcast(FP8X4), wq_plane[h][:], wq_bf[h][:])
             for e in range(4):
                 bank = banks[2 * h + e // 2]
@@ -137,62 +137,63 @@ def tile_attend_lookahead_delivered_lean_kernel(tc, query, keys_words, keys_scal
         def scatter(h, e, engine):
             move(engine, df[e][:].indirect(lists[3][:, h * LIST_COLS : (h + 1) * LIST_COLS]), dl[h, e // 2][:, (e % 2) * HALF : (e % 2 + 1) * HALF])
 
-        faded = [tile([P, M], F32, f"faded{e}") for e in range(4)]
+        faded = {}
         res = [tile([P, M], F32, f"res{e}") for e in range(4)]
 
         def fade_old(e):
-            nc.vector.tensor_tensor(faded[e][:], old_sb[e][:], fade_all[:], ALU.mult)
+            if e % 2 == 0:
+                faded.setdefault(e // 2, tile([P, 2 * M], F32, ("early", "late")[e // 2]))
+            nc.gpsimd.tensor_tensor(faded[e // 2][:, (e % 2) * M : (e % 2 + 1) * M], old_sb[e][:], fade_all[:], ALU.mult)
 
         def finish(e, pieces):
             width = M // pieces
             for c in range(pieces):
                 cols = slice(c * width, (c + 1) * width)
-                nc.vector.tensor_tensor(res[e][:, cols], faded[e][:, cols], df[e][:, cols], ALU.add)
+                nc.vector.tensor_tensor(res[e][:, cols], faded[e // 2][:, (e % 2) * M + c * width : (e % 2) * M + (c + 1) * width], df[e][:, cols], ALU.add)
                 nc.sync.dma_start(out[e * P : (e + 1) * P, cols], res[e][:, cols])
 
-        def unit(h, r):
-            gather(h, r, 1, "S")
-            gather(h, r, 2, "S")
-            gather(h, r, 0, "V")
         for r in range(PACK):
             score(r, 0, "S")
             score(r, 1, "V")
             if r >= 1:
-                unit(0, r - 1)
-            if r >= 2:
-                weigh(0, r - 2)
-        unit(0, 3)
-        interleave(m_bf[:], m_raw[:].rearrange("p j c -> p (j c)"), E)
-        weigh(0, 2)
-        nc.vector.quantize_mx(m_codes[:].bitcast(FP8X4), m_plane[:], m_bf[:])
-        unit(1, 0)
-        weigh(0, 3)
-        unit(1, 1)
-        deliver(0)
-        weigh(1, 0)
-        unit(1, 2)
-        weigh(1, 1)
-        unit(1, 3)
-        weigh(1, 2)
-        evacuate(0, 0, "S")
-        scatter(0, 0, "S")
-        weigh(1, 3)
-        deliver(1)
+                gather(0, r - 1, 1, "S")
+                gather_own(r - 1)
+                gather(0, r - 1, 2, "S")
+        nc.gpsimd.tensor_scalar(m_bf[:].rearrange("p (c j) -> p c j", j=PACK), m_raw[:].rearrange("p j c -> p c j"), 1.0, 0.0, ALU.mult, ALU.add)
         fade_old(0)
-        scatter(0, 1, "S")
-        evacuate(1, 0, "V")
-        scatter(1, 0, "V")
-        evacuate(0, 1, "S")
-        scatter(1, 1, "S")
-        finish(0, 1)
         fade_old(1)
-        scatter(0, 2, "S")
-        evacuate(1, 1, "V")
-        finish(1, 1)
-        scatter(1, 2, "S")
+        gather(0, 3, 1, "S")
+        gather_own(3)
+        gather(0, 3, 2, "S")
+        for r in range(PACK):
+            gather(1, r, 1, "S")
+            gather(1, r, 2, "S")
+        nc.vector.quantize_mx(m_codes[:].bitcast(FP8X4), m_plane[:], m_bf[:])
+        for h in range(2):
+            weigh_max(h, 0)
+            weigh_max(h, 1)
+            for r in range(PACK):
+                weigh_sum(h, r)
+            for r in range(PACK):
+                weigh_scale(h, r)
+            interleave(wq_bf[h][:], wq_rows[h][:], HALF)
+            deliver(h)
+            if h == 0:
+                evacuate(0, 0, "S")
+                scatter(0, 0, "S")
+                scatter(0, 1, "S")
+                evacuate(0, 1, "S")
+                scatter(0, 2, "S")
+                scatter(0, 3, "S")
         fade_old(2)
         fade_old(3)
-        scatter(0, 3, "S")
-        finish(2, 1)
+        evacuate(1, 0, "V")
+        evacuate(1, 1, "V")
+        scatter(1, 0, "V")
+        scatter(1, 1, "V")
+        scatter(1, 2, "S")
         scatter(1, 3, "S")
+        finish(0, 1)
+        finish(1, 1)
+        finish(2, 1)
         finish(3, 2)

@@ -39,13 +39,15 @@ def tile_attend_lookahead_delivered_lean_kernel(tc, query, keys_words, keys_scal
 
         key_plane = tile([P, T], U8, "key_plane")
         nc.vector.memset(key_plane[:].bitcast(I32), 0)
-        q_raw = [tile([P, PACK, Q // 2], F32, f"q_raw{u}") for u in range(2)]
-        for u in range(2):
-            nc.sync.dma_start(q_raw[u][:], query.rearrange("(p j) c -> p j c", j=PACK)[:, :, u * (Q // 2) : (u + 1) * (Q // 2)])
-        for g in range(4):
-            nc.scalar.dma_start(key_plane[32 * g : 32 * g + 4, :].bitcast(I32), keys_scales[0, 4 * g : 4 * g + 4, :].bitcast(I32))
+        q_cuts = (0, 192, 384, Q)
+        q_raw = [tile([P, PACK, q_cuts[u + 1] - q_cuts[u]], F32, f"q_raw{u}") for u in range(3)]
+        for u in range(3):
+            nc.sync.dma_start(q_raw[u][:], query.rearrange("(p j) c -> p j c", j=PACK)[:, :, q_cuts[u] : q_cuts[u + 1]])
         key_words = tile([P, T], U32, "key_words")
-        nc.sync.dma_start(key_words[:].bitcast(I32), keys_words[0].rearrange("p n t -> p (n t)").bitcast(I32))
+        words_hbm = keys_words[0].rearrange("p n t -> p (n t)").bitcast(I32)
+        nc.sync.dma_start(key_words[:].bitcast(I32), words_hbm)
+        for g in range(4):
+            nc.sync.dma_start(key_plane[32 * g : 32 * g + 4, :].bitcast(I32), keys_scales[0, 4 * g : 4 * g + 4, :].bitcast(I32))
         lists = [tile([P, I // 16], U16, f"list{k}") for k in range(4)]
         for k, src in ((1, offs2), (0, offs), (2, offs3)):
             nc.sync.dma_start(lists[k][:], src)
@@ -65,12 +67,12 @@ def tile_attend_lookahead_delivered_lean_kernel(tc, query, keys_words, keys_scal
 
         df = [tile([P, M], F32, f"df{e}") for e in range(4)]
         for e in range(4):
-            nc.vector.memset(df[e][:], 0.0)
+            (nc.vector, nc.gpsimd)[e // 2].memset(df[e][:], 0.0)
 
         q_bf = tile([P, Q * PACK], BF16, "q_bf")
         q_view = q_bf[:].rearrange("p (r m j) -> p m j r", r=PACK, j=PACK)
-        for u in range(2):
-            nc.vector.tensor_copy(q_view[:, u * 64 : (u + 1) * 64], q_raw[u][:].rearrange("p j (m r) -> p m j r", r=PACK))
+        for u in range(3):
+            nc.vector.tensor_copy(q_view[:, q_cuts[u] // PACK : q_cuts[u + 1] // PACK], q_raw[u][:].rearrange("p j (m r) -> p m j r", r=PACK))
         q_codes = [tile([P, P], U32, f"q_codes{r}") for r in range(PACK)]
         q_plane = [tile([P, P], U8, f"q_plane{r}") for r in range(PACK)]
         for r in range(PACK):
@@ -86,7 +88,7 @@ def tile_attend_lookahead_delivered_lean_kernel(tc, query, keys_words, keys_scal
                                 rhs=key_words[:, cols].bitcast(FP8X4), rhs_scale=key_plane[:, cols], start=True, stop=True)
             move(engine, a[r][:, cols], bank[:])
 
-        own = [tile([P, I], F32, f"own{r}") for r in range(PACK)]
+        own = {}
         got = {}
         wq_rows = [tile([P, PACK * HALF], BF16, f"wq_rows{h}") for h in range(2)]
         wq_bf = [tile([P, PACK * HALF], BF16, ("wq_bf0", "late")[h]) for h in range(2)]
@@ -97,20 +99,22 @@ def tile_attend_lookahead_delivered_lean_kernel(tc, query, keys_words, keys_scal
 
         def gather(h, r, k, engine):
             if r == 0:
-                got.setdefault((h, k), tile([P, PACK * HALF], F32, (f"got{k}", ("key_words", "key_plane")[k - 1])[h]))
+                got.setdefault((h, k), tile([P, PACK * HALF], F32, {(0, 1): "got", (0, 2): "key_words", (1, 1): "key_plane", (1, 2): "q_plane3"}[h, k]))
             move(engine, got[h, k][:, r * HALF : (r + 1) * HALF], a[r][:].indirect(lists[k][:, h * LIST_COLS : (h + 1) * LIST_COLS]))
 
-        def gather_own(r):
-            nc.vector.tensor_copy(own[r][:], a[r][:].indirect(lists[0][:]))
+        def gather_own(h, r):
+            if r == 0:
+                own.setdefault(h, tile([P, PACK * HALF], F32, ("own", "wq_rows0")[h]))
+            nc.vector.tensor_copy(own[h][:, r * HALF : (r + 1) * HALF], a[r][:].indirect(lists[0][:, h * LIST_COLS : (h + 1) * LIST_COLS]))
 
         def weigh_max(h, pair):
             if pair == 0:
-                best.setdefault(h, tile([P, PACK * HALF], F32, ("m_bf", "wq_bf0")[h]))
+                best.setdefault(h, tile([P, PACK * HALF], F32, ("best", "wq_bf0")[h]))
             cols = slice(2 * pair * HALF, 2 * (pair + 1) * HALF)
             nc.vector.tensor_tensor(best[h][:, cols], got[h, 1][:, cols], got[h, 2][:, cols], ALU.max)
 
         def weigh_sum(h, r):
-            nc.vector.scalar_tensor_tensor(w[h, r][:], best[h][:, r * HALF : (r + 1) * HALF], lam4[:, r : r + 1], own[r][:, h * HALF : (h + 1) * HALF], ALU.mult, ALU.add)
+            nc.vector.scalar_tensor_tensor(w[h, r][:], best[h][:, r * HALF : (r + 1) * HALF], lam4[:, r : r + 1], own[h][:, r * HALF : (r + 1) * HALF], ALU.mult, ALU.add)
 
         def weigh_scale(h, r):
             nc.vector.tensor_scalar(wq_rows[h][:, r * HALF : (r + 1) * HALF], w[h, r][:], qs4[:, r : r + 1], None, ALU.mult)
@@ -118,7 +122,6 @@ def tile_attend_lookahead_delivered_lean_kernel(tc, query, keys_words, keys_scal
         def interleave(dst, src, width):
             nc.vector.tensor_copy(dst.rearrange("p (c i j) -> p c j i", i=4, j=PACK), src.rearrange("p (j c i) -> p c j i", i=4, j=PACK))
 
-        m_bf = tile([P, E * PACK], BF16, "m_bf")
         m_codes = tile([P, E], U32, "m_codes")
         m_plane = tile([P, E], U8, "m_plane")
         dl = {(h, e): tile([P, 2 * HALF], F32, f"dl{h}{e}") for h in range(2) for e in range(2)}
@@ -137,19 +140,16 @@ def tile_attend_lookahead_delivered_lean_kernel(tc, query, keys_words, keys_scal
         def scatter(h, e, engine):
             move(engine, df[e][:].indirect(lists[3][:, h * LIST_COLS : (h + 1) * LIST_COLS]), dl[h, e // 2][:, (e % 2) * HALF : (e % 2 + 1) * HALF])
 
-        faded = {}
         res = [tile([P, M], F32, f"res{e}") for e in range(4)]
 
         def fade_old(e):
-            if e % 2 == 0:
-                faded.setdefault(e // 2, tile([P, 2 * M], F32, ("early", "late")[e // 2]))
-            nc.gpsimd.tensor_tensor(faded[e // 2][:, (e % 2) * M : (e % 2 + 1) * M], old_sb[e][:], fade_all[:], ALU.mult)
+            nc.vector.tensor_tensor(faded[:, e * M : (e + 1) * M], old_sb[e][:], fade_all[:], ALU.mult)
 
         def finish(e, pieces):
             width = M // pieces
             for c in range(pieces):
                 cols = slice(c * width, (c + 1) * width)
-                nc.vector.tensor_tensor(res[e][:, cols], faded[e // 2][:, (e % 2) * M + c * width : (e % 2) * M + (c + 1) * width], df[e][:, cols], ALU.add)
+                nc.vector.tensor_tensor(res[e][:, cols], faded[:, e * M + c * width : e * M + (c + 1) * width], df[e][:, cols], ALU.add)
                 nc.sync.dma_start(out[e * P : (e + 1) * P, cols], res[e][:, cols])
 
         for r in range(PACK):
@@ -157,20 +157,21 @@ def tile_attend_lookahead_delivered_lean_kernel(tc, query, keys_words, keys_scal
             score(r, 1, "V")
             if r >= 1:
                 gather(0, r - 1, 1, "S")
-                gather_own(r - 1)
-                gather(0, r - 1, 2, "S")
-        nc.gpsimd.tensor_scalar(m_bf[:].rearrange("p (c j) -> p c j", j=PACK), m_raw[:].rearrange("p j c -> p c j"), 1.0, 0.0, ALU.mult, ALU.add)
-        fade_old(0)
-        fade_old(1)
+                gather_own(0, r - 1)
         gather(0, 3, 1, "S")
-        gather_own(3)
-        gather(0, 3, 2, "S")
-        for r in range(PACK):
-            gather(1, r, 1, "S")
-            gather(1, r, 2, "S")
+        gather_own(0, 3)
+        m_bf = tile([P, E * PACK], BF16, "q_codes3")
+        interleave(m_bf[:], m_raw[:].rearrange("p j c -> p (j c)"), E)
+        for h, k in ((0, 2), (1, 1), (1, 2)):
+            for r in range(PACK):
+                gather(h, r, k, "S")
+        weigh_max(0, 0)
         nc.vector.quantize_mx(m_codes[:].bitcast(FP8X4), m_plane[:], m_bf[:])
         for h in range(2):
-            weigh_max(h, 0)
+            if h == 1:
+                for r in range(PACK):
+                    gather_own(1, r)
+                weigh_max(1, 0)
             weigh_max(h, 1)
             for r in range(PACK):
                 weigh_sum(h, r)
@@ -178,22 +179,16 @@ def tile_attend_lookahead_delivered_lean_kernel(tc, query, keys_words, keys_scal
                 weigh_scale(h, r)
             interleave(wq_bf[h][:], wq_rows[h][:], HALF)
             deliver(h)
-            if h == 0:
-                evacuate(0, 0, "S")
-                scatter(0, 0, "S")
-                scatter(0, 1, "S")
-                evacuate(0, 1, "S")
-                scatter(0, 2, "S")
-                scatter(0, 3, "S")
+            for pair in range(2):
+                evacuate(h, pair, "SV"[h])
+                scatter(h, 2 * pair, "S")
+                scatter(h, 2 * pair + 1, "S")
+        faded = tile([P, 4 * M], F32, "late")
+        fade_old(0)
+        fade_old(1)
         fade_old(2)
-        fade_old(3)
-        evacuate(1, 0, "V")
-        evacuate(1, 1, "V")
-        scatter(1, 0, "V")
-        scatter(1, 1, "V")
-        scatter(1, 2, "S")
-        scatter(1, 3, "S")
         finish(0, 1)
+        fade_old(3)
         finish(1, 1)
         finish(2, 1)
         finish(3, 2)

@@ -39,10 +39,8 @@ def tile_attend_lookahead_delivered_lean_kernel(tc, query, keys_words, keys_scal
 
         key_plane = tile([P, T], U8, "key_plane")
         nc.vector.memset(key_plane[:].bitcast(I32), 0)
-        q_cuts = (0, 192, 384, Q)
-        q_raw = [tile([P, PACK, q_cuts[u + 1] - q_cuts[u]], F32, f"q_raw{u}") for u in range(3)]
-        for u in range(3):
-            nc.sync.dma_start(q_raw[u][:], query.rearrange("(p j) c -> p j c", j=PACK)[:, :, q_cuts[u] : q_cuts[u + 1]])
+        q_raw = tile([P, PACK, Q], F32, "q_raw")
+        nc.sync.dma_start(q_raw[:], query.rearrange("(p j) c -> p j c", j=PACK))
         key_words = tile([P, T], U32, "key_words")
         words_hbm = keys_words[0].rearrange("p n t -> p (n t)").bitcast(I32)
         nc.sync.dma_start(key_words[:].bitcast(I32), words_hbm)
@@ -71,12 +69,20 @@ def tile_attend_lookahead_delivered_lean_kernel(tc, query, keys_words, keys_scal
 
         q_bf = tile([P, Q * PACK], BF16, "q_bf")
         q_view = q_bf[:].rearrange("p (r m j) -> p m j r", r=PACK, j=PACK)
-        for u in range(3):
-            nc.vector.tensor_copy(q_view[:, q_cuts[u] // PACK : q_cuts[u + 1] // PACK], q_raw[u][:].rearrange("p j (m r) -> p m j r", r=PACK))
         q_codes = [tile([P, P], U32, f"q_codes{r}") for r in range(PACK)]
         q_plane = [tile([P, P], U8, f"q_plane{r}") for r in range(PACK)]
-        for r in range(PACK):
+
+        def deal(r):
+            nc.vector.tensor_copy(q_view[:, :, :, r : r + 2], q_raw[:].rearrange("p j (m r) -> p m j r", r=PACK)[:, :, :, r : r + 2])
+
+        def quantize_query(r):
             nc.vector.quantize_mx(q_codes[r][:].bitcast(FP8X4), q_plane[r][:], q_bf[:, r * 512 : (r + 1) * 512])
+
+        deal(0)
+        quantize_query(0)
+        deal(2)
+        for r in range(1, PACK):
+            quantize_query(r)
 
         a = [tile([P, T], F32, f"a{r}") for r in range(PACK)]
         banks = [ps.tile([P, BANK], F32, name=f"bank{b}") for b in range(8)]

@@ -1,6 +1,7 @@
 from contextlib import ExitStack
 
 import concourse.mybir as mybir
+from concourse.masks import make_identity
 
 D, T, I, Q, E, M = 512, 1024, 512, 512, 512, 1024
 FLOPS = 2 * D * Q * T + 2 * Q * E * I
@@ -19,182 +20,222 @@ P = 128
 PACK = 4
 BANK = 512
 HALF = I // 2
-LIST_COLS = HALF // 16
+PER_COL = 16
+E_TILES = E // P
+FADE_BANK = 4
+SHARE = 256
+LAST_CUT = HALF // 2
 
 
-def tile_attend_lookahead_delivered_lean_kernel(tc, query, keys_words, keys_scales, lam, qs, msgs, old, fade, offs, offs2, offs3, offs4, out):
+def tile_attend_lookahead_delivered_lean_kernel(
+    tc, query, keys_words, keys_scales, lam, qs, msgs, old, fade, offs, offs2, offs3, offs4, out
+):
     nc = tc.nc
     with ExitStack() as ctx:
         sb = ctx.enter_context(tc.tile_pool(name="sb", bufs=1))
         ps = ctx.enter_context(tc.psum_pool(name="ps", bufs=1))
 
-        def tile(shape, dtype, name):
-            return sb.tile(shape, dtype, name=name, align_bytes=64)
+        def tile(shape, dtype, buffer):
+            return sb.tile(shape, dtype, name=buffer, align_bytes=64)
 
-        def move(engine, dst, src):
-            if engine == "S":
-                nc.scalar.activation(dst, src, COPY)
-            else:
-                nc.vector.tensor_copy(dst, src)
+        def on_scalar(dst, src):
+            nc.scalar.activation(dst, src, COPY)
+
+        def on_vector(dst, src):
+            nc.vector.tensor_copy(dst, src)
+
+        def part(n, width):
+            return slice(n * width, (n + 1) * width)
 
         key_plane = tile([P, T], U8, "key_plane")
         nc.vector.memset(key_plane[:].bitcast(I32), 0)
         q_raw = tile([P, PACK, Q], F32, "q_raw")
         nc.sync.dma_start(q_raw[:], query.rearrange("(p j) c -> p j c", j=PACK))
         key_words = tile([P, T], U32, "key_words")
-        words_hbm = keys_words[0].rearrange("p n t -> p (n t)").bitcast(I32)
-        nc.sync.dma_start(key_words[:].bitcast(I32), words_hbm)
+        nc.sync.dma_start(key_words[:].bitcast(I32), keys_words[0].rearrange("p n t -> p (n t)").bitcast(I32))
         for g in range(4):
-            nc.sync.dma_start(key_plane[32 * g : 32 * g + 4, :].bitcast(I32), keys_scales[0, 4 * g : 4 * g + 4, :].bitcast(I32))
-        lists = [tile([P, I // 16], U16, f"list{k}") for k in range(4)]
-        for k, src in ((1, offs2), (0, offs), (2, offs3)):
-            nc.sync.dma_start(lists[k][:], src)
+            nc.sync.dma_start(key_plane[32 * g : 32 * g + 4, :].bitcast(I32), keys_scales[0, part(g, 4), :].bitcast(I32))
+        own_list, first_list, second_list, place_list = (tile([P, I // PER_COL], U16, f"list{k}") for k in range(4))
+        nc.sync.dma_start(first_list[:], offs2)
+        nc.sync.dma_start(own_list[:], offs)
+        nc.sync.dma_start(second_list[:], offs3)
         lam4 = tile([P, PACK], F32, "lam4")
         qs4 = tile([P, PACK], F32, "qs4")
         m_raw = tile([P, PACK, E], F32, "m_raw")
         nc.sync.dma_start(m_raw[:], msgs.rearrange("(p j) c -> p j c", j=PACK))
-        fade_all = tile([P, M], F32, "fade_all")
-        nc.sync.dma_start(fade_all[:], fade.rearrange("o m -> (o m)").partition_broadcast(P))
-        old_sb = [tile([P, M], F32, f"old{e}") for e in range(4)]
-        for e in range(4):
-            nc.sync.dma_start(old_sb[e][:], old[e * P : (e + 1) * P, :])
-            if e == 1:
-                nc.sync.dma_start(lam4[:], lam.rearrange("(p j) o -> p (j o)", j=PACK))
-                nc.sync.dma_start(qs4[:], qs.rearrange("(p j) o -> p (j o)", j=PACK))
-                nc.sync.dma_start(lists[3][:], offs4)
+        nc.sync.dma_start(lam4[:], lam.rearrange("(p j) o -> p (j o)", j=PACK))
+        nc.sync.dma_start(qs4[:], qs.rearrange("(p j) o -> p (j o)", j=PACK))
+        nc.sync.dma_start(place_list[:], offs4)
+        fade_cols = tile([P, 2, PACK], F32, "fade_cols")
+        nc.sync.dma_start(fade_cols[:], fade.rearrange("o (b p c) -> p (o b) c", b=2, c=PACK))
+        fade_rows = tile([P, M], F32, "fade_rows")
+        nc.sync.dma_start(fade_rows[:], fade.rearrange("o m -> (o m)").partition_broadcast(P))
+        old_sb = [tile([P, M], F32, f"old{e}") for e in range(E_TILES)]
+        for e in range(E_TILES):
+            nc.sync.dma_start(old_sb[e][:], old[part(e, P), :])
 
-        df = [tile([P, M], F32, f"df{e}") for e in range(4)]
-        for e in range(4):
+        df = [tile([P, M], F32, f"df{e}") for e in range(E_TILES)]
+        for e in range(E_TILES):
             (nc.vector, nc.gpsimd)[e // 2].memset(df[e][:], 0.0)
+        ident = tile([P, P], F32, "ident")
+        make_identity(nc, ident[:])
 
         q_bf = tile([P, Q * PACK], BF16, "q_bf")
-        q_view = q_bf[:].rearrange("p (r m j) -> p m j r", r=PACK, j=PACK)
         q_codes = [tile([P, P], U32, f"q_codes{r}") for r in range(PACK)]
         q_plane = [tile([P, P], U8, f"q_plane{r}") for r in range(PACK)]
 
-        def deal(r):
-            nc.vector.tensor_copy(q_view[:, :, :, r : r + 2], q_raw[:].rearrange("p j (m r) -> p m j r", r=PACK)[:, :, :, r : r + 2])
+        def deal(pair):
+            nc.vector.tensor_copy(
+                q_bf[:].rearrange("p (r m j) -> p m j r", r=PACK, j=PACK)[:, :, :, part(pair, 2)],
+                q_raw[:].rearrange("p j (m r) -> p m j r", r=PACK)[:, :, :, part(pair, 2)],
+            )
 
         def quantize_query(r):
-            nc.vector.quantize_mx(q_codes[r][:].bitcast(FP8X4), q_plane[r][:], q_bf[:, r * 512 : (r + 1) * 512])
+            nc.vector.quantize_mx(q_codes[r][:].bitcast(FP8X4), q_plane[r][:], q_bf[:, part(r, P * PACK)])
 
         deal(0)
         quantize_query(0)
-        deal(2)
+        deal(1)
         for r in range(1, PACK):
             quantize_query(r)
 
         a = [tile([P, T], F32, f"a{r}") for r in range(PACK)]
         banks = [ps.tile([P, BANK], F32, name=f"bank{b}") for b in range(8)]
 
-        def score(r, b, engine):
-            bank = banks[2 * r + b]
-            cols = slice(b * BANK, (b + 1) * BANK)
-            nc.tensor.matmul_mx(bank[:], lhsT=q_codes[r][:].bitcast(FP8X4), lhsT_scale=q_plane[r][:],
-                                rhs=key_words[:, cols].bitcast(FP8X4), rhs_scale=key_plane[:, cols], start=True, stop=True)
-            move(engine, a[r][:, cols], bank[:])
+        def score(r, b, move):
+            cols = part(b, BANK)
+            nc.tensor.matmul_mx(
+                banks[2 * r + b][:],
+                lhsT=q_codes[r][:].bitcast(FP8X4),
+                lhsT_scale=q_plane[r][:],
+                rhs=key_words[:, cols].bitcast(FP8X4),
+                rhs_scale=key_plane[:, cols],
+                start=True,
+                stop=True,
+            )
+            move(a[r][:, cols], banks[2 * r + b][:])
 
-        own = {}
-        got = {}
-        wq_rows = [tile([P, PACK * HALF], BF16, f"wq_rows{h}") for h in range(2)]
-        wq_bf = [tile([P, PACK * HALF], BF16, ("wq_bf0", "late")[h]) for h in range(2)]
-        wq_codes = [tile([P, HALF], U32, f"wq_codes{h}") for h in range(2)]
-        wq_plane = [tile([P, HALF], U8, f"wq_plane{h}") for h in range(2)]
-        best = {}
-        w = {(h, r): tile([P, HALF], F32, f"w{h}{r}") for h in range(2) for r in range(PACK)}
+        def look_up(dst, offsets, h, r, move):
+            move(dst[:, part(r, HALF)], a[r][:].indirect(offsets[:, part(h, HALF // PER_COL)]))
 
-        def gather(h, r, k, engine):
-            if r == 0:
-                got.setdefault((h, k), tile([P, PACK * HALF], F32, {(0, 1): "got", (0, 2): "key_words", (1, 1): "key_plane", (1, 2): "q_plane3"}[h, k]))
-            move(engine, got[h, k][:, r * HALF : (r + 1) * HALF], a[r][:].indirect(lists[k][:, h * LIST_COLS : (h + 1) * LIST_COLS]))
+        own = [tile([P, PACK * HALF], F32, "own")]
+        first = [tile([P, PACK * HALF], F32, "first")]
+        for r in range(PACK + 1):
+            if r < PACK:
+                score(r, 0, on_scalar)
+                score(r, 1, on_vector)
+            if r > 0:
+                look_up(first[0], first_list, 0, r - 1, on_scalar)
+                look_up(own[0], own_list, 0, r - 1, on_vector)
 
-        def gather_own(h, r):
-            if r == 0:
-                own.setdefault(h, tile([P, PACK * HALF], F32, ("own", "wq_rows0")[h]))
-            nc.vector.tensor_copy(own[h][:, r * HALF : (r + 1) * HALF], a[r][:].indirect(lists[0][:, h * LIST_COLS : (h + 1) * LIST_COLS]))
+        for b in range(2):
+            for c in range(PACK):
+                nc.tensor.transpose(banks[FADE_BANK + b][:, part(c, P)], fade_cols[:, b, c : c + 1].to_broadcast([P, P]), ident[:])
 
-        def weigh_max(h, pair):
-            if pair == 0:
-                best.setdefault(h, tile([P, PACK * HALF], F32, ("best", "wq_bf0")[h]))
-            cols = slice(2 * pair * HALF, 2 * (pair + 1) * HALF)
-            nc.vector.tensor_tensor(best[h][:, cols], got[h, 1][:, cols], got[h, 2][:, cols], ALU.max)
+        def interleave(dst, src):
+            nc.vector.tensor_copy(
+                dst.rearrange("p (c i j) -> p c j i", i=4, j=PACK), src.rearrange("p (j c i) -> p c j i", i=4, j=PACK)
+            )
 
-        def weigh_sum(h, r):
-            nc.vector.scalar_tensor_tensor(w[h, r][:], best[h][:, r * HALF : (r + 1) * HALF], lam4[:, r : r + 1], own[h][:, r * HALF : (r + 1) * HALF], ALU.mult, ALU.add)
-
-        def weigh_scale(h, r):
-            nc.vector.tensor_scalar(wq_rows[h][:, r * HALF : (r + 1) * HALF], w[h, r][:], qs4[:, r : r + 1], None, ALU.mult)
-
-        def interleave(dst, src, width):
-            nc.vector.tensor_copy(dst.rearrange("p (c i j) -> p c j i", i=4, j=PACK), src.rearrange("p (j c i) -> p c j i", i=4, j=PACK))
+        m_bf = tile([P, E * PACK], BF16, "q_codes3")
+        second = [tile([P, PACK * HALF], F32, "key_words")]
+        first.append(tile([P, PACK * HALF], F32, "key_plane"))
+        second.append(tile([P, PACK * HALF], F32, "q_plane3"))
+        interleave(m_bf[:], m_raw[:].rearrange("p j c -> p (j c)"))
+        for dst, offsets, h in ((second[0], second_list, 0), (first[1], first_list, 1), (second[1], second_list, 1)):
+            for r in range(PACK):
+                look_up(dst, offsets, h, r, on_scalar)
 
         m_codes = tile([P, E], U32, "m_codes")
         m_plane = tile([P, E], U8, "m_plane")
-        dl = {(h, e): tile([P, 2 * HALF], F32, f"dl{h}{e}") for h in range(2) for e in range(2)}
+        best = [tile([P, PACK * HALF], F32, "best")]
+        w = [tile([P, PACK * HALF], F32, f"w{h}") for h in range(2)]
+        wq_rows = [tile([P, PACK * HALF], BF16, f"wq_rows{h}") for h in range(2)]
+        wq_bf = [tile([P, PACK * HALF], BF16, f"wq_bf{h}") for h in range(2)]
+        wq_codes = [tile([P, HALF], U32, f"wq_codes{h}") for h in range(2)]
+        wq_plane = [tile([P, HALF], U8, f"wq_plane{h}") for h in range(2)]
+        dl = [[tile([P, 2 * HALF], F32, f"dl{h}{pair}") for pair in range(2)] for h in range(2)]
+
+        def larger_follower(h, pair):
+            cols = part(pair, 2 * HALF)
+            nc.vector.tensor_tensor(best[h][:, cols], first[h][:, cols], second[h][:, cols], ALU.max)
+
+        def weigh(h):
+            for r in range(PACK):
+                cols = part(r, HALF)
+                nc.vector.scalar_tensor_tensor(w[h][:, cols], best[h][:, cols], lam4[:, r : r + 1], own[h][:, cols], ALU.mult, ALU.add)
+            for r in range(PACK):
+                cols = part(r, HALF)
+                nc.vector.tensor_scalar(wq_rows[h][:, cols], w[h][:, cols], qs4[:, r : r + 1], None, ALU.mult)
+            interleave(wq_bf[h][:], wq_rows[h][:])
+            nc.vector.quantize_mx(wq_codes[h][:].bitcast(FP8X4), wq_plane[h][:], wq_bf[h][:])
 
         def deliver(h):
-            nc.vector.quantize_mx(wq_codes[h][:].bitcast(FP8X4), wq_plane[h][:], wq_bf[h][:])
-            for e in range(4):
-                bank = banks[2 * h + e // 2]
-                cols = slice(e * P, (e + 1) * P)
-                nc.tensor.matmul_mx(bank[:, (e % 2) * HALF : (e % 2 + 1) * HALF], lhsT=m_codes[:, cols].bitcast(FP8X4), lhsT_scale=m_plane[:, cols],
-                                    rhs=wq_codes[h][:].bitcast(FP8X4), rhs_scale=wq_plane[h][:], start=True, stop=True)
+            for e in range(E_TILES):
+                nc.tensor.matmul_mx(
+                    banks[2 * h + e // 2][:, part(e % 2, HALF)],
+                    lhsT=m_codes[:, part(e, P)].bitcast(FP8X4),
+                    lhsT_scale=m_plane[:, part(e, P)],
+                    rhs=wq_codes[h][:].bitcast(FP8X4),
+                    rhs_scale=wq_plane[h][:],
+                    start=True,
+                    stop=True,
+                )
 
-        def evacuate(h, pair, engine):
-            move(engine, dl[h, pair][:], banks[2 * h + pair][:])
+        def scatter(h, e, move, lo=0, hi=HALF):
+            offsets = place_list[:, (h * HALF + lo) // PER_COL : (h * HALF + hi) // PER_COL]
+            move(df[e][:].indirect(offsets), dl[h][e // 2][:, (e % 2) * HALF + lo : (e % 2) * HALF + hi])
 
-        def scatter(h, e, engine):
-            move(engine, df[e][:].indirect(lists[3][:, h * LIST_COLS : (h + 1) * LIST_COLS]), dl[h, e // 2][:, (e % 2) * HALF : (e % 2 + 1) * HALF])
-
-        res = [tile([P, M], F32, f"res{e}") for e in range(4)]
-
-        def fade_old(e):
-            nc.vector.tensor_tensor(faded[:, e * M : (e + 1) * M], old_sb[e][:], fade_all[:], ALU.mult)
-
-        def finish(e, pieces):
-            width = M // pieces
-            for c in range(pieces):
-                cols = slice(c * width, (c + 1) * width)
-                nc.vector.tensor_tensor(res[e][:, cols], faded[:, e * M + c * width : e * M + (c + 1) * width], df[e][:, cols], ALU.add)
-                nc.sync.dma_start(out[e * P : (e + 1) * P, cols], res[e][:, cols])
-
-        for r in range(PACK):
-            score(r, 0, "S")
-            score(r, 1, "V")
-            if r >= 1:
-                gather(0, r - 1, 1, "S")
-                gather_own(0, r - 1)
-        gather(0, 3, 1, "S")
-        gather_own(0, 3)
-        m_bf = tile([P, E * PACK], BF16, "q_codes3")
-        interleave(m_bf[:], m_raw[:].rearrange("p j c -> p (j c)"), E)
-        for h, k in ((0, 2), (1, 1), (1, 2)):
-            for r in range(PACK):
-                gather(h, r, k, "S")
-        weigh_max(0, 0)
+        larger_follower(0, 0)
         nc.vector.quantize_mx(m_codes[:].bitcast(FP8X4), m_plane[:], m_bf[:])
-        for h in range(2):
-            if h == 1:
-                for r in range(PACK):
-                    gather_own(1, r)
-                weigh_max(1, 0)
-            weigh_max(h, 1)
-            for r in range(PACK):
-                weigh_sum(h, r)
-            for r in range(PACK):
-                weigh_scale(h, r)
-            interleave(wq_bf[h][:], wq_rows[h][:], HALF)
-            deliver(h)
-            for pair in range(2):
-                evacuate(h, pair, "SV"[h])
-                scatter(h, 2 * pair, "S")
-                scatter(h, 2 * pair + 1, "S")
-        faded = tile([P, 4 * M], F32, "late")
-        fade_old(0)
-        fade_old(1)
-        fade_old(2)
-        finish(0, 1)
-        fade_old(3)
-        finish(1, 1)
-        finish(2, 1)
-        finish(3, 2)
+        larger_follower(0, 1)
+        weigh(0)
+        deliver(0)
+        for e in range(E_TILES):
+            if e % 2 == 0:
+                on_scalar(dl[0][e // 2][:], banks[e // 2][:])
+            scatter(0, e, on_scalar)
+
+        own.append(tile([P, PACK * HALF], F32, "wq_rows0"))
+        best.append(tile([P, PACK * HALF], F32, "wq_bf0"))
+        for r in range(PACK):
+            look_up(own[1], own_list, 1, r, on_vector)
+        for pair in range(2):
+            larger_follower(1, pair)
+        weigh(1)
+        deliver(1)
+        for e in range(E_TILES - 1):
+            if e % 2 == 0:
+                on_vector(dl[1][e // 2][:], banks[2 + e // 2][:])
+            scatter(1, e, on_scalar)
+
+        faded = tile([P, E_TILES * M], F32, "wq_bf1")
+
+        def fade_on_gpsimd(e, lo):
+            nc.gpsimd.tensor_tensor(faded[:, e * M + lo : (e + 1) * M], old_sb[e][:, lo:], fade_rows[:, lo:], ALU.mult)
+
+        def fade_on_vector(e, b, width):
+            lo = b * BANK
+            nc.vector.tensor_tensor(
+                faded[:, e * M + lo : e * M + lo + width].rearrange("p (k c) -> p k c", c=PACK),
+                old_sb[e][:, lo : lo + width].rearrange("p (k c) -> p k c", c=PACK),
+                banks[FADE_BANK + b][:].rearrange("p (c k) -> p k c", c=PACK)[:, : width // PACK, :],
+                ALU.mult,
+            )
+
+        fade_on_gpsimd(2, SHARE)
+        fade_on_gpsimd(3, 0)
+        for e in range(2):
+            for b in range(2):
+                fade_on_vector(e, b, BANK)
+        fade_on_vector(2, 0, SHARE)
+        scatter(1, E_TILES - 1, on_vector, 0, LAST_CUT)
+        scatter(1, E_TILES - 1, on_scalar, LAST_CUT, HALF)
+
+        res = [tile([P, M], F32, f"res{e}") for e in range(E_TILES)]
+        for e in range(E_TILES):
+            pieces = 2 if e == E_TILES - 1 else 1
+            for c in range(pieces):
+                cols = part(c, M // pieces)
+                nc.vector.tensor_tensor(res[e][:, cols], faded[:, part(e, M)][:, cols], df[e][:, cols], ALU.add)
+                nc.sync.dma_start(out[part(e, P), cols], res[e][:, cols])

from contextlib import ExitStack

import concourse.mybir as mybir
from concourse.masks import make_identity

D, T, I, Q, E, M = 512, 1024, 512, 512, 512, 1024
FLOPS = 2 * D * Q * T + 2 * Q * E * I

F32 = mybir.dt.float32
BF16 = mybir.dt.bfloat16
I32 = mybir.dt.int32
U32 = mybir.dt.uint32
U16 = mybir.dt.uint16
U8 = mybir.dt.uint8
FP8X4 = mybir.dt.float8_e4m3fn_x4
ALU = mybir.AluOpType
COPY = mybir.ActivationFunctionType.Copy

P = 128
PACK = 4
BANK = 512
HALF = I // 2
PER_COL = 16
E_TILES = E // P
FADE_BANK = 4
SHARE = 256
LAST_CUT = HALF // 2


def tile_attend_lookahead_delivered_lean_kernel(
    tc, query, keys_words, keys_scales, lam, qs, msgs, old, fade, offs, offs2, offs3, offs4, out
):
    nc = tc.nc
    with ExitStack() as ctx:
        sb = ctx.enter_context(tc.tile_pool(name="sb", bufs=1))
        ps = ctx.enter_context(tc.psum_pool(name="ps", bufs=1))

        def tile(shape, dtype, buffer):
            return sb.tile(shape, dtype, name=buffer, align_bytes=64)

        def on_scalar(dst, src):
            nc.scalar.activation(dst, src, COPY)

        def on_vector(dst, src):
            nc.vector.tensor_copy(dst, src)

        def part(n, width):
            return slice(n * width, (n + 1) * width)

        key_plane = tile([P, T], U8, "key_plane")
        nc.vector.memset(key_plane[:].bitcast(I32), 0)
        q_raw = tile([P, PACK, Q], F32, "q_raw")
        nc.sync.dma_start(q_raw[:], query.rearrange("(p j) c -> p j c", j=PACK))
        key_words = tile([P, T], U32, "key_words")
        nc.sync.dma_start(key_words[:].bitcast(I32), keys_words[0].rearrange("p n t -> p (n t)").bitcast(I32))
        for g in range(4):
            nc.sync.dma_start(key_plane[32 * g : 32 * g + 4, :].bitcast(I32), keys_scales[0, part(g, 4), :].bitcast(I32))
        own_list, first_list, second_list, place_list = (tile([P, I // PER_COL], U16, f"list{k}") for k in range(4))
        nc.sync.dma_start(first_list[:], offs2)
        nc.sync.dma_start(own_list[:], offs)
        nc.sync.dma_start(second_list[:], offs3)
        lam4 = tile([P, PACK], F32, "lam4")
        qs4 = tile([P, PACK], F32, "qs4")
        m_raw = tile([P, PACK, E], F32, "m_raw")
        nc.sync.dma_start(m_raw[:], msgs.rearrange("(p j) c -> p j c", j=PACK))
        nc.sync.dma_start(lam4[:], lam.rearrange("(p j) o -> p (j o)", j=PACK))
        nc.sync.dma_start(qs4[:], qs.rearrange("(p j) o -> p (j o)", j=PACK))
        nc.sync.dma_start(place_list[:], offs4)
        fade_cols = tile([P, 2, PACK], F32, "fade_cols")
        nc.sync.dma_start(fade_cols[:], fade.rearrange("o (b p c) -> p (o b) c", b=2, c=PACK))
        fade_rows = tile([P, M], F32, "fade_rows")
        nc.sync.dma_start(fade_rows[:], fade.rearrange("o m -> (o m)").partition_broadcast(P))
        old_sb = [tile([P, M], F32, f"old{e}") for e in range(E_TILES)]
        for e in range(E_TILES):
            nc.sync.dma_start(old_sb[e][:], old[part(e, P), :])

        df = [tile([P, M], F32, f"df{e}") for e in range(E_TILES)]
        for e in range(E_TILES):
            (nc.vector, nc.gpsimd)[e // 2].memset(df[e][:], 0.0)
        ident = tile([P, P], F32, "ident")
        make_identity(nc, ident[:])

        q_bf = tile([P, Q * PACK], BF16, "q_bf")
        q_codes = [tile([P, P], U32, f"q_codes{r}") for r in range(PACK)]
        q_plane = [tile([P, P], U8, f"q_plane{r}") for r in range(PACK)]

        def deal(pair):
            nc.vector.tensor_copy(
                q_bf[:].rearrange("p (r m j) -> p m j r", r=PACK, j=PACK)[:, :, :, part(pair, 2)],
                q_raw[:].rearrange("p j (m r) -> p m j r", r=PACK)[:, :, :, part(pair, 2)],
            )

        def quantize_query(r):
            nc.vector.quantize_mx(q_codes[r][:].bitcast(FP8X4), q_plane[r][:], q_bf[:, part(r, P * PACK)])

        deal(0)
        quantize_query(0)
        deal(1)
        for r in range(1, PACK):
            quantize_query(r)

        a = [tile([P, T], F32, f"a{r}") for r in range(PACK)]
        banks = [ps.tile([P, BANK], F32, name=f"bank{b}") for b in range(8)]

        def score(r, b, move):
            cols = part(b, BANK)
            nc.tensor.matmul_mx(
                banks[2 * r + b][:],
                lhsT=q_codes[r][:].bitcast(FP8X4),
                lhsT_scale=q_plane[r][:],
                rhs=key_words[:, cols].bitcast(FP8X4),
                rhs_scale=key_plane[:, cols],
                start=True,
                stop=True,
            )
            move(a[r][:, cols], banks[2 * r + b][:])

        def look_up(dst, offsets, h, r, move):
            move(dst[:, part(r, HALF)], a[r][:].indirect(offsets[:, part(h, HALF // PER_COL)]))

        own = [tile([P, PACK * HALF], F32, "own")]
        first = [tile([P, PACK * HALF], F32, "first")]
        for r in range(PACK + 1):
            if r < PACK:
                score(r, 0, on_scalar)
                score(r, 1, on_vector)
            if r > 0:
                look_up(first[0], first_list, 0, r - 1, on_scalar)
                look_up(own[0], own_list, 0, r - 1, on_vector)

        for b in range(2):
            for c in range(PACK):
                nc.tensor.transpose(banks[FADE_BANK + b][:, part(c, P)], fade_cols[:, b, c : c + 1].to_broadcast([P, P]), ident[:])

        def interleave(dst, src):
            nc.vector.tensor_copy(
                dst.rearrange("p (c i j) -> p c j i", i=4, j=PACK), src.rearrange("p (j c i) -> p c j i", i=4, j=PACK)
            )

        m_bf = tile([P, E * PACK], BF16, "q_codes3")
        second = [tile([P, PACK * HALF], F32, "key_words")]
        first.append(tile([P, PACK * HALF], F32, "key_plane"))
        second.append(tile([P, PACK * HALF], F32, "q_plane3"))
        interleave(m_bf[:], m_raw[:].rearrange("p j c -> p (j c)"))
        for dst, offsets, h in ((second[0], second_list, 0), (first[1], first_list, 1), (second[1], second_list, 1)):
            for r in range(PACK):
                look_up(dst, offsets, h, r, on_scalar)

        m_codes = tile([P, E], U32, "m_codes")
        m_plane = tile([P, E], U8, "m_plane")
        best = [tile([P, PACK * HALF], F32, "best")]
        w = [tile([P, PACK * HALF], F32, f"w{h}") for h in range(2)]
        wq_rows = [tile([P, PACK * HALF], BF16, f"wq_rows{h}") for h in range(2)]
        wq_bf = [tile([P, PACK * HALF], BF16, f"wq_bf{h}") for h in range(2)]
        wq_codes = [tile([P, HALF], U32, f"wq_codes{h}") for h in range(2)]
        wq_plane = [tile([P, HALF], U8, f"wq_plane{h}") for h in range(2)]
        dl = [[tile([P, 2 * HALF], F32, f"dl{h}{pair}") for pair in range(2)] for h in range(2)]

        def larger_follower(h, pair):
            cols = part(pair, 2 * HALF)
            nc.vector.tensor_tensor(best[h][:, cols], first[h][:, cols], second[h][:, cols], ALU.max)

        def weigh(h):
            for r in range(PACK):
                cols = part(r, HALF)
                nc.vector.scalar_tensor_tensor(w[h][:, cols], best[h][:, cols], lam4[:, r : r + 1], own[h][:, cols], ALU.mult, ALU.add)
            for r in range(PACK):
                cols = part(r, HALF)
                nc.vector.tensor_scalar(wq_rows[h][:, cols], w[h][:, cols], qs4[:, r : r + 1], None, ALU.mult)
            interleave(wq_bf[h][:], wq_rows[h][:])
            nc.vector.quantize_mx(wq_codes[h][:].bitcast(FP8X4), wq_plane[h][:], wq_bf[h][:])

        def deliver(h):
            for e in range(E_TILES):
                nc.tensor.matmul_mx(
                    banks[2 * h + e // 2][:, part(e % 2, HALF)],
                    lhsT=m_codes[:, part(e, P)].bitcast(FP8X4),
                    lhsT_scale=m_plane[:, part(e, P)],
                    rhs=wq_codes[h][:].bitcast(FP8X4),
                    rhs_scale=wq_plane[h][:],
                    start=True,
                    stop=True,
                )

        def scatter(h, e, move, lo=0, hi=HALF):
            offsets = place_list[:, (h * HALF + lo) // PER_COL : (h * HALF + hi) // PER_COL]
            move(df[e][:].indirect(offsets), dl[h][e // 2][:, (e % 2) * HALF + lo : (e % 2) * HALF + hi])

        larger_follower(0, 0)
        nc.vector.quantize_mx(m_codes[:].bitcast(FP8X4), m_plane[:], m_bf[:])
        larger_follower(0, 1)
        weigh(0)
        deliver(0)
        for e in range(E_TILES):
            if e % 2 == 0:
                on_scalar(dl[0][e // 2][:], banks[e // 2][:])
            scatter(0, e, on_scalar)

        own.append(tile([P, PACK * HALF], F32, "wq_rows0"))
        best.append(tile([P, PACK * HALF], F32, "wq_bf0"))
        for r in range(PACK):
            look_up(own[1], own_list, 1, r, on_vector)
        for pair in range(2):
            larger_follower(1, pair)
        weigh(1)
        deliver(1)
        for e in range(E_TILES - 1):
            if e % 2 == 0:
                on_vector(dl[1][e // 2][:], banks[2 + e // 2][:])
            scatter(1, e, on_scalar)

        faded = tile([P, E_TILES * M], F32, "wq_bf1")

        def fade_on_gpsimd(e, lo):
            nc.gpsimd.tensor_tensor(faded[:, e * M + lo : (e + 1) * M], old_sb[e][:, lo:], fade_rows[:, lo:], ALU.mult)

        def fade_on_vector(e, b, width):
            lo = b * BANK
            nc.vector.tensor_tensor(
                faded[:, e * M + lo : e * M + lo + width].rearrange("p (k c) -> p k c", c=PACK),
                old_sb[e][:, lo : lo + width].rearrange("p (k c) -> p k c", c=PACK),
                banks[FADE_BANK + b][:].rearrange("p (c k) -> p k c", c=PACK)[:, : width // PACK, :],
                ALU.mult,
            )

        fade_on_gpsimd(2, SHARE)
        fade_on_gpsimd(3, 0)
        for e in range(2):
            for b in range(2):
                fade_on_vector(e, b, BANK)
        fade_on_vector(2, 0, SHARE)
        scatter(1, E_TILES - 1, on_vector, 0, LAST_CUT)
        scatter(1, E_TILES - 1, on_scalar, LAST_CUT, HALF)

        res = [tile([P, M], F32, f"res{e}") for e in range(E_TILES)]
        for e in range(E_TILES):
            pieces = 2 if e == E_TILES - 1 else 1
            for c in range(pieces):
                cols = part(c, M // pieces)
                nc.vector.tensor_tensor(res[e][:, cols], faded[:, part(e, M)][:, cols], df[e][:, cols], ALU.add)
                nc.sync.dma_start(out[part(e, P), cols], res[e][:, cols])
